import numpy as np
import ml_dtypes


def mxq(x, axis, fmt="e4m3"):
    dtype, down = {"e4m3": (ml_dtypes.float8_e4m3fn, 7), "e5m2": (ml_dtypes.float8_e5m2, 14)}[fmt]
    v = np.moveaxis(np.asarray(x, np.float32).astype(ml_dtypes.bfloat16).astype(np.float64), axis, -1)
    blocks = v.reshape(v.shape[:-1] + (-1, 32))
    amax = np.abs(blocks).max(-1, keepdims=True)
    byte = np.maximum(np.where(amax > 0, np.frexp(amax)[1] - 1 + 127, 0) - down, 1)
    scale = np.exp2(byte - 127.0)
    codes = (blocks / scale).astype(np.float32).astype(dtype).astype(np.float64)
    return np.moveaxis((codes * scale).reshape(v.shape), -1, axis)


WIDE = False


def mx_kscale(k):
    if not WIDE:
        return np.ones(k)
    levels = np.array([30, -30])
    if k % 512:
        return np.exp2(np.random.permutation(np.resize(levels, k // 32))).repeat(32)
    a = np.empty((k // 512, 16))
    for p in range(k // 512):
        a[p, :8] = np.random.permutation(np.resize(levels, 8))
        for g in range(8):
            far = levels[np.abs(levels - a[p, g]) >= 10]
            a[p, g + 8] = far[np.random.randint(len(far))]
    return np.exp2(a.ravel()).repeat(32)


def f64(x):
    return np.asarray(x).astype(np.float64)


def striped(idx):
    return np.tile(np.asarray(idx).reshape(-1, 16).T, (8, 1)).astype(np.uint16)


def unstriped(offs):
    return offs[:16].T.reshape(-1).astype(np.int64)


E2M1 = np.array([0.0, 0.5, 1.0, 1.5, 2.0, 3.0, 4.0, 6.0, -0.0, -0.5, -1.0, -1.5, -2.0, -3.0, -4.0, -6.0])


def pack_weight(w, fmt):
    k, n = w.shape
    w = f64(np.asarray(w, np.float32).astype(ml_dtypes.bfloat16)).reshape(k // 32, 32, n)
    amax = np.abs(w).max(1)
    if fmt in ("e4m3", "e5m2"):
        byte = np.frexp(amax)[1] - 1 + 127 - (7 if fmt == "e4m3" else 14)
    else:
        mant, ex = np.frexp(amax / 6.0)
        byte = np.where(mant > 0.5, ex, ex - 1) + 127
    byte = np.clip(np.where(amax > 0, byte, 1), 1, 254)
    scaled = (w * np.exp2(127.0 - byte)[:, None, :]).reshape(k, n).astype(np.float32)
    by_word = np.ascontiguousarray(scaled.reshape(k // 512, 128, 4, n).transpose(0, 1, 3, 2))
    if fmt in ("e4m3", "e5m2"):
        words = by_word.astype(ml_dtypes.float8_e4m3fn if fmt == "e4m3" else ml_dtypes.float8_e5m2).view(np.uint8)
    else:
        c = by_word.astype(ml_dtypes.float4_e2m1fn).view(np.uint8) & 0xF
        words = (c[..., 0::2] | (c[..., 1::2] << 4)).reshape(k // 512, 128, 2 * n)
    return np.ascontiguousarray(words), np.ascontiguousarray(byte.astype(np.uint8).reshape(k // 512, 16, n))


def unpack_weight(words, scales, fmt):
    g, _, n = scales.shape
    words = np.ascontiguousarray(words).reshape(g, 128, n, -1)
    if fmt in ("e4m3", "e5m2"):
        vals = words.view(ml_dtypes.float8_e4m3fn if fmt == "e4m3" else ml_dtypes.float8_e5m2).astype(np.float64)
    else:
        nib = np.empty((g, 128, n, 4), np.uint8)
        nib[..., 0::2] = words & 0xF
        nib[..., 1::2] = words >> 4
        vals = E2M1[nib]
    vals = vals * np.repeat(np.exp2(scales.astype(np.float64) - 127.0), 8, axis=1)[..., None]
    return vals.transpose(0, 1, 3, 2).reshape(g * 512, n)


def sigmoid(v):
    return 1.0 / (1.0 + np.exp(-v))


def sgn(shape):
    return np.random.uniform(0.5, 2.0, shape) * np.where(np.random.standard_normal(shape) < 0, -1.0, 1.0)


K, T, J, R, C, D, O, N = 512, 2048, 256, 512, 512, 512, 128, 256


def setup_inputs():
    n = np.random.standard_normal
    idx = np.random.permutation(T)[:J]
    idx2 = np.random.permutation(T)[:J]
    idx3 = np.random.permutation(C)[:J]
    idx4 = np.random.permutation(D)[:J]
    idx5 = np.random.permutation(C)[:O]
    idx6 = np.random.permutation(C)[:O]
    idx7 = np.random.permutation(D)[:O]
    fk = mx_kscale(K)
    fr = mx_kscale(R)
    xtp = pack_weight(n((K, T)) / fk[:, None], "e5m2")
    wp = pack_weight(n((K, R)) * 1 / np.sqrt(K) * fk[:, None], "e2m1")
    w2p = pack_weight(n((K, R)) * 1 / np.sqrt(K) * fk[:, None], "e4m3")
    wbp = pack_weight(n((R, N)) * 1 / np.sqrt(R) / fr[:, None], "e2m1")
    return {
        "xt_words": xtp[0],
        "xt_scales": xtp[1],
        "w_words": wp[0],
        "w_scales": wp[1],
        "w2_words": w2p[0],
        "w2_scales": w2p[1],
        "sa": (np.random.uniform(0.5, 1.6, (R, 1)) * fr[:, None]).astype(np.float32),
        "sb": (np.random.uniform(0.5, 1.6, (R, 1)) * fr[:, None]).astype(np.float32),
        "sg": (sgn((R, 1))).astype(np.float32),
        "bg": (np.random.uniform(-2.0, 2.0, (R, 1))).astype(np.float32),
        "wb_words": wbp[0],
        "wb_scales": wbp[1],
        "offs": striped(idx),
        "offs2": striped(idx2),
        "offs3": striped(idx3),
        "offs4": striped(idx4),
        "offs5": striped(idx5),
        "offs6": striped(idx6),
        "offs7": striped(idx7),
    }


def reference(xt_words, xt_scales, w_words, w_scales, w2_words, w2_scales, sa, sb, sg, bg, wb_words, wb_scales, offs, offs2, offs3, offs4, offs5, offs6, offs7):
    idx = unstriped(offs)
    idx2 = unstriped(offs2)
    idx3 = unstriped(offs3)
    idx4 = unstriped(offs4)
    idx5 = unstriped(offs5)
    idx6 = unstriped(offs6)
    idx7 = unstriped(offs7)
    xtu = unpack_weight(xt_words, xt_scales, "e5m2")
    wu = unpack_weight(w_words, w_scales, "e2m1")
    w2u = unpack_weight(w2_words, w2_scales, "e4m3")
    wbu = unpack_weight(wb_words, wb_scales, "e2m1")
    xtidxg = xtu[:, idx]
    a = wu.T @ xtidxg
    xtidx2g = xtu[:, idx2]
    b = w2u.T @ xtidx2g
    pw = np.zeros((R, C))
    pw[:, idx3] = a
    pv = np.zeros((R, D))
    pv[:, idx4] = b
    u1 = pw[:, idx5] * f64(sa) * sigmoid(pw[:, idx6] * f64(sg) + f64(bg))
    hid = np.maximum(u1, pv[:, idx7] * f64(sb))
    hidq = mxq(hid, 0, "e4m3")
    y = wbu.T @ hidq
    return y

@@ -1,0 +1,228 @@
+from contextlib import ExitStack
+
+import concourse.mybir as mybir
+
+K, T, J, R, C, O, N = 512, 2048, 256, 512, 512, 128, 256
+FLOPS = 2 * K * R * J * 2 + 2 * R * N * O
+
+F32 = mybir.dt.float32
+BF16 = mybir.dt.bfloat16
+I32 = mybir.dt.int32
+U32 = mybir.dt.uint32
+U16 = mybir.dt.uint16
+U8 = mybir.dt.uint8
+E4M3 = mybir.dt.float8_e4m3fn_x4
+E5M2 = mybir.dt.float8_e5m2_x4
+E2M1 = mybir.dt.float4_e2m1fn_x4
+ACT = mybir.ActivationFunctionType
+ALU = mybir.AluOpType
+
+P = 128
+PACK = 4
+QUAD = 32
+
+
+def tile_list_gatedboards_ahead_one_plain_kernel(
+    tc, xt_words, xt_scales, w_words, w_scales, w2_words, w2_scales, sa, sb, sg, bg,
+    wb_words, wb_scales, offs, offs2, offs3, offs4, offs5, offs6, offs7, out,
+):
+    nc = tc.nc
+    with ExitStack() as ctx:
+        keep = ctx.enter_context(tc.tile_pool(name="keep", bufs=1))
+        psum = ctx.enter_context(tc.psum_pool(name="psum", bufs=1))
+
+        def sb_tile(name, shape, dtype, tag=None):
+            return keep.tile(shape, dtype, name=name, tag=tag or name, align_bytes=64)
+
+        def load_list(name, src):
+            lst = keep.tile(list(src.shape), U16, name=name)
+            nc.sync.dma_start(lst[:], src)
+            return lst
+
+        def load_rows(name, src):
+            col = keep.tile([P, PACK], F32, name=name)
+            nc.sync.dma_start(col[:], src.rearrange("(p t) one -> p (t one)", t=PACK))
+            return col
+
+        def load_scale_rows(plane, src):
+            for q in range(PACK):
+                nc.sync.dma_start(
+                    plane[QUAD * q : QUAD * q + PACK, :].bitcast(I32),
+                    src[0, PACK * q : PACK * q + PACK, :].bitcast(I32),
+                )
+
+        def stage_scales(name, src, queue):
+            staged = sb_tile(name, [PACK, PACK, R // 4], I32)
+            queue.dma_start(staged[:], src[0].bitcast(I32).rearrange("(q r) c -> r q c", r=PACK))
+            return staged
+
+        def deal_scales(name, spread):
+            dealt = sb_tile(name, [P, R], U8)
+            nc.gpsimd.tensor_copy(
+                dealt[:].rearrange("p (t m) -> p t m", t=PACK),
+                spread[:].rearrange("p (m t) -> p t m", t=PACK),
+            )
+            return dealt
+
+        warm = keep.tile([P, 2], F32, name="warm")
+        nc.gpsimd.memset(warm[:, 0:1], 0.0)
+        x_scales = sb_tile("x_scales", [P, T], U8)
+        nc.vector.memset(x_scales[:].bitcast(I32), 0)
+        w_spread = sb_tile("w_spread", [P, R], U8)
+        nc.vector.memset(w_spread[:].bitcast(I32), 0)
+        w2_spread = sb_tile("w2_spread", [P, R], U8)
+        nc.gpsimd.memset(w2_spread[:].bitcast(I32), 0)
+
+        x_staged = [sb_tile("x_staged%d" % h, [P, 2, T // 4], I32) for h in range(2)]
+        x_rows = xt_scales[0].bitcast(I32).rearrange("(h q r) c -> h r q c", h=2, q=2)
+        nc.sync.dma_start(x_staged[0][0:PACK, :, :], x_rows[0])
+        nc.scalar.dma_start(x_staged[1][2 * QUAD : 2 * QUAD + PACK, :, :], x_rows[1])
+        list1 = load_list("list1", offs)
+        w_staged = stage_scales("w_staged", w_scales, nc.scalar)
+        w_raw = sb_tile("w_raw", [P, 2 * R], U8)
+        nc.scalar.dma_start(w_raw[:].bitcast(I32), w_words[0].bitcast(I32))
+        x_words = sb_tile("x_words", [P, T], U32)
+        nc.scalar.dma_start(x_words[:].bitcast(I32), xt_words[0].rearrange("p c t -> p (c t)").bitcast(I32))
+        nc.scalar.activation(warm[:, 1:2], warm[:, 0:1], ACT.Sigmoid)
+        list3 = load_list("list3", offs3)
+        w2_raw = sb_tile("w2_raw", [P, R], U32)
+        nc.scalar.dma_start(w2_raw[:].bitcast(I32), w2_words[0].rearrange("p c t -> p (c t)").bitcast(I32))
+        list2 = load_list("list2", offs2)
+        load_scale_rows(w2_spread, w2_scales)
+        list6 = load_list("list6", offs6)
+        list5 = load_list("list5", offs5)
+        sg_col = load_rows("sg_col", sg)
+        bg_col = load_rows("bg_col", bg)
+        sa_col = load_rows("sa_col", sa)
+        list4 = load_list("list4", offs4)
+        list7 = load_list("list7", offs7)
+        sb_col = load_rows("sb_col", sb)
+        wb_codes = sb_tile("wb_codes", [P, 2 * N], U8)
+        nc.sync.dma_start(wb_codes[:].bitcast(I32), wb_words[0].bitcast(I32))
+
+        board_w = [keep.tile([P, C], F32, name="board_w%d" % t) for t in range(PACK)]
+        for t in range(PACK):
+            (nc.vector if t < 2 else nc.gpsimd).memset(board_w[t][:], 0.0)
+
+        for q in range(PACK):
+            nc.vector.tensor_copy(w_spread[QUAD * q : QUAD * q + PACK, :].bitcast(I32), w_staged[:, q, :])
+        w_dealt_scales = deal_scales("w_dealt_scales", w_spread)
+        for q in range(PACK):
+            src = 2 * QUAD * (q // 2)
+            nc.vector.tensor_copy(x_scales[QUAD * q : QUAD * q + PACK, :].bitcast(I32), x_staged[q // 2][src : src + PACK, q % 2, :])
+        w_dealt = sb_tile("w_dealt", [P, 2 * R], U8)
+        nc.scalar.copy(
+            w_dealt[:].bitcast(U16).rearrange("p (t m) -> p t m", t=PACK),
+            w_raw[:].bitcast(U16).rearrange("p (m t) -> p t m", t=PACK),
+        )
+
+        x1_scales = sb_tile("x1_scales", [P, J], U8)
+        nc.vector.tensor_copy(x1_scales[:], x_scales[:].indirect(list1[:]))
+        x1_words = sb_tile("x1_words", [P, J], U32)
+        nc.vector.tensor_copy(x1_words[:], x_words[:].indirect(list1[:]))
+        x2_scales = sb_tile("x2_scales", [P, J], U8)
+        nc.vector.tensor_copy(x2_scales[:], x_scales[:].indirect(list2[:]))
+        w2_dealt_scales = deal_scales("w2_dealt_scales", w2_spread)
+
+        w2_dealt = sb_tile("w2_dealt", [P, R], U32)
+        nc.gpsimd.tensor_copy(
+            w2_dealt[:].rearrange("p (t m) -> p t m", t=PACK),
+            w2_raw[:].rearrange("p (m t) -> p t m", t=PACK),
+        )
+        x2_words = sb_tile("x2_words", [P, J], U32)
+        nc.vector.tensor_copy(x2_words[:], x_words[:].indirect(list2[:]))
+
+        wb_plane = sb_tile("wb_plane", [P, N], U8)
+        nc.gpsimd.memset(wb_plane[:].bitcast(I32), 0)
+        load_scale_rows(wb_plane, wb_scales)
+
+        a_sums = [psum.tile([P, J], F32, name="a_sums%d" % t, tag="bank%d" % t) for t in range(PACK)]
+        b_sums = [psum.tile([P, 2, J], F32, name="b_sums%d" % h) for h in range(2)]
+        for t in (1, 0, 3, 2):
+            nc.tensor.matmul_mx(
+                out=a_sums[t][:],
+                lhsT=w_dealt[:, 2 * P * t : 2 * P * (t + 1)].bitcast(E2M1),
+                lhsT_scale=w_dealt_scales[:, P * t : P * (t + 1)],
+                rhs=x1_words[:].bitcast(E5M2), rhs_scale=x1_scales[:], start=True, stop=True,
+            )
+        for t in range(PACK):
+            nc.tensor.matmul_mx(
+                out=b_sums[t // 2][:, t % 2, :],
+                lhsT=w2_dealt[:, P * t : P * (t + 1)].bitcast(E4M3),
+                lhsT_scale=w2_dealt_scales[:, P * t : P * (t + 1)],
+                rhs=x2_words[:].bitcast(E5M2), rhs_scale=x2_scales[:], start=True, stop=True,
+            )
+        spent = ["w_dealt", "w_dealt_scales", "w2_dealt", "w2_dealt_scales"]
+        board_v = [sb_tile("board_v%d" % t, [P, C], F32, tag=spent[t]) for t in range(PACK)]
+        for t in range(PACK):
+            nc.gpsimd.memset(board_v[t][:], 0.0)
+
+        a_rows = [keep.tile([P, J], F32, name="a_rows%d" % t) for t in range(PACK)]
+        b_rows = [keep.tile([P, 2, J], F32, name="b_rows%d" % h) for h in range(2)]
+        first = keep.tile([P, PACK, O], F32, name="first")
+        gate = keep.tile([P, PACK, O], F32, name="gate")
+        second = keep.tile([P, PACK, O], F32, name="second")
+
+        def put(engine, board, lst, rows):
+            if engine == "vector":
+                nc.vector.tensor_copy(board[:].indirect(lst[:]), rows)
+            else:
+                nc.scalar.activation(board[:].indirect(lst[:]), rows, ACT.Copy)
+
+        def look_w(t):
+            nc.scalar.activation(gate[:, t, :], board_w[t][:].indirect(list6[:]), ACT.Sigmoid,
+                                 bias=bg_col[:, t : t + 1], scale=sg_col[:, t : t + 1])
+            nc.scalar.activation(first[:, t, :], board_w[t][:].indirect(list5[:]), ACT.Copy,
+                                 scale=sa_col[:, t : t + 1])
+
+        def look_v(t):
+            nc.scalar.activation(second[:, t, :], board_v[t][:].indirect(list7[:]), ACT.Copy,
+                                 scale=sb_col[:, t : t + 1])
+
+        nc.scalar.copy(a_rows[1][:], a_sums[1][:])
+        nc.scalar.copy(a_rows[0][:], a_sums[0][:])
+        put("scalar", board_w[1], list3, a_rows[1][:])
+        put("vector", board_w[0], list3, a_rows[0][:])
+        nc.scalar.copy(a_rows[3][:], a_sums[3][:])
+        nc.vector.tensor_copy(a_rows[2][:], a_sums[2][:])
+        put("scalar", board_w[3], list3, a_rows[3][:])
+        put("vector", board_w[2], list3, a_rows[2][:])
+        nc.vector.tensor_copy(b_rows[0][:], b_sums[0][:])
+        nc.vector.tensor_copy(b_rows[1][:], b_sums[1][:])
+        for t in range(PACK):
+            look_w(t)
+        put("vector", board_v[0], list4, b_rows[0][:, 0, :])
+        put("vector", board_v[1], list4, b_rows[0][:, 1, :])
+        put("scalar", board_v[2], list4, b_rows[1][:, 0, :])
+        put("vector", board_v[3], list4, b_rows[1][:, 1, :])
+        gated = keep.tile([P, PACK, O], F32, name="gated")
+        nc.gpsimd.tensor_tensor(gated[:], first[:], gate[:], ALU.mult)
+        for t in range(PACK):
+            look_v(t)
+
+        hid = sb_tile("hid", [P, O * PACK], BF16)
+        nc.vector.tensor_tensor(
+            hid[:].rearrange("p (c i t) -> p c t i", i=4, t=PACK),
+            gated[:].rearrange("p t (c i) -> p c t i", i=4),
+            second[:].rearrange("p t (c i) -> p c t i", i=4),
+            ALU.max,
+        )
+        hid_codes = sb_tile("hid_codes", [P, O], U32)
+        hid_scales = sb_tile("hid_scales", [P, O], U8)
+        nc.vector.quantize_mx(out=hid_codes[:].bitcast(E4M3), scales=hid_scales[:], in_=hid[:])
+
+        for h in range(N // P):
+            y_sums = psum.tile([P, O], F32, name="y_sums%d" % h, tag="bank%d" % h)
+            nc.tensor.matmul_mx(
+                out=y_sums[:],
+                lhsT=wb_codes[:, 2 * P * h : 2 * P * (h + 1)].bitcast(E2M1),
+                lhsT_scale=wb_plane[:, P * h : P * (h + 1)],
+                rhs=hid_codes[:].bitcast(E4M3), rhs_scale=hid_scales[:], start=True, stop=True,
+            )
+            y_rows = keep.tile([P, O], F32, name="y_rows%d" % h)
+            if h == 0:
+                nc.scalar.copy(y_rows[:], y_sums[:])
+                nc.scalar.dma_start(out[P * h : P * (h + 1), :], y_rows[:])
+            else:
+                nc.vector.tensor_copy(y_rows[:], y_sums[:])
+                nc.sync.dma_start(out[P * h : P * (h + 1), :], y_rows[:])

@@ -137,7 +137,8 @@ def tile_list_gatedboards_ahead_one_plain_kernel(
         load_scale_rows(wb_plane, wb_scales)
 
         a_sums = [psum.tile([P, J], F32, name="a_sums%d" % t, tag="bank%d" % t) for t in range(PACK)]
-        b_sums = [psum.tile([P, 2, J], F32, name="b_sums%d" % h) for h in range(2)]
+        b_pair = psum.tile([P, 2, J], F32, name="b_pair")
+        b_sums = [b_pair[:, 0, :], b_pair[:, 1, :]] + [psum.tile([P, J], F32, name="b_sums%d" % t)[:] for t in (2, 3)]
         for t in (1, 0, 3, 2):
             nc.tensor.matmul_mx(
                 out=a_sums[t][:],
@@ -147,7 +148,7 @@ def tile_list_gatedboards_ahead_one_plain_kernel(
             )
         for t in range(PACK):
             nc.tensor.matmul_mx(
-                out=b_sums[t // 2][:, t % 2, :],
+                out=b_sums[t],
                 lhsT=w2_dealt[:, P * t : P * (t + 1)].bitcast(E4M3),
                 lhsT_scale=w2_dealt_scales[:, P * t : P * (t + 1)],
                 rhs=x2_words[:].bitcast(E5M2), rhs_scale=x2_scales[:], start=True, stop=True,
@@ -158,7 +159,8 @@ def tile_list_gatedboards_ahead_one_plain_kernel(
             nc.gpsimd.memset(board_v[t][:], 0.0)
 
         a_rows = [keep.tile([P, J], F32, name="a_rows%d" % t) for t in range(PACK)]
-        b_rows = [keep.tile([P, 2, J], F32, name="b_rows%d" % h) for h in range(2)]
+        b_pair_rows = keep.tile([P, 2, J], F32, name="b_pair_rows")
+        b_rows = [b_pair_rows[:, 0, :], b_pair_rows[:, 1, :]] + [keep.tile([P, J], F32, name="b_rows%d" % t)[:] for t in (2, 3)]
         first = keep.tile([P, PACK, O], F32, name="first")
         gate = keep.tile([P, PACK, O], F32, name="gate")
         second = keep.tile([P, PACK, O], F32, name="second")
@@ -187,26 +189,25 @@ def tile_list_gatedboards_ahead_one_plain_kernel(
         nc.vector.tensor_copy(a_rows[2][:], a_sums[2][:])
         put("scalar", board_w[3], list3, a_rows[3][:])
         put("vector", board_w[2], list3, a_rows[2][:])
-        nc.vector.tensor_copy(b_rows[0][:], b_sums[0][:])
-        nc.vector.tensor_copy(b_rows[1][:], b_sums[1][:])
+        nc.vector.tensor_copy(b_pair_rows[:], b_pair[:])
+        nc.vector.tensor_copy(b_rows[3], b_sums[3])
+        nc.scalar.copy(b_rows[2], b_sums[2])
         for t in range(PACK):
             look_w(t)
-        put("vector", board_v[0], list4, b_rows[0][:, 0, :])
-        put("vector", board_v[1], list4, b_rows[0][:, 1, :])
-        put("scalar", board_v[2], list4, b_rows[1][:, 0, :])
-        put("vector", board_v[3], list4, b_rows[1][:, 1, :])
+        put("vector", board_v[0], list4, b_rows[0])
+        put("vector", board_v[1], list4, b_rows[1])
+        put("scalar", board_v[2], list4, b_rows[2])
+        put("vector", board_v[3], list4, b_rows[3])
         gated = keep.tile([P, PACK, O], F32, name="gated")
         nc.gpsimd.tensor_tensor(gated[:], first[:], gate[:], ALU.mult)
         for t in range(PACK):
             look_v(t)
 
+        larger = keep.tile([P, PACK, O], F32, name="larger")
+        nc.vector.tensor_tensor(larger[:, : PACK - 1, :], gated[:, : PACK - 1, :], second[:, : PACK - 1, :], ALU.max)
+        nc.vector.tensor_tensor(larger[:, PACK - 1, :], gated[:, PACK - 1, :], second[:, PACK - 1, :], ALU.max)
         hid = sb_tile("hid", [P, O * PACK], BF16)
-        nc.vector.tensor_tensor(
-            hid[:].rearrange("p (c i t) -> p c t i", i=4, t=PACK),
-            gated[:].rearrange("p t (c i) -> p c t i", i=4),
-            second[:].rearrange("p t (c i) -> p c t i", i=4),
-            ALU.max,
-        )
+        nc.vector.tensor_copy(hid[:].rearrange("p (o t) -> p o t", t=PACK), larger[:].rearrange("p t o -> p o t"))
         hid_codes = sb_tile("hid_codes", [P, O], U32)
         hid_scales = sb_tile("hid_scales", [P, O], U8)
         nc.vector.quantize_mx(out=hid_codes[:].bitcast(E4M3), scales=hid_scales[:], in_=hid[:])

from contextlib import ExitStack

import concourse.mybir as mybir

K, T, J, R, C, O, N = 512, 2048, 256, 512, 512, 128, 256
FLOPS = 2 * K * R * J * 2 + 2 * R * N * O

F32 = mybir.dt.float32
BF16 = mybir.dt.bfloat16
I32 = mybir.dt.int32
U32 = mybir.dt.uint32
U16 = mybir.dt.uint16
U8 = mybir.dt.uint8
E4M3 = mybir.dt.float8_e4m3fn_x4
E5M2 = mybir.dt.float8_e5m2_x4
E2M1 = mybir.dt.float4_e2m1fn_x4
ACT = mybir.ActivationFunctionType
ALU = mybir.AluOpType

P = 128
PACK = 4
QUAD = 32


def tile_list_gatedboards_ahead_one_plain_kernel(
    tc, xt_words, xt_scales, w_words, w_scales, w2_words, w2_scales, sa, sb, sg, bg,
    wb_words, wb_scales, offs, offs2, offs3, offs4, offs5, offs6, offs7, out,
):
    nc = tc.nc
    with ExitStack() as ctx:
        keep = ctx.enter_context(tc.tile_pool(name="keep", bufs=1))
        psum = ctx.enter_context(tc.psum_pool(name="psum", bufs=1))

        def sb_tile(name, shape, dtype, tag=None):
            return keep.tile(shape, dtype, name=name, tag=tag or name, align_bytes=64)

        def load_list(name, src):
            lst = keep.tile(list(src.shape), U16, name=name)
            nc.sync.dma_start(lst[:], src)
            return lst

        def load_rows(name, src):
            col = keep.tile([P, PACK], F32, name=name)
            nc.sync.dma_start(col[:], src.rearrange("(p t) one -> p (t one)", t=PACK))
            return col

        def load_scale_rows(plane, src):
            for q in range(PACK):
                nc.sync.dma_start(
                    plane[QUAD * q : QUAD * q + PACK, :].bitcast(I32),
                    src[0, PACK * q : PACK * q + PACK, :].bitcast(I32),
                )

        def stage_scales(name, src, queue):
            staged = sb_tile(name, [PACK, PACK, R // 4], I32)
            queue.dma_start(staged[:], src[0].bitcast(I32).rearrange("(q r) c -> r q c", r=PACK))
            return staged

        def deal_scales(name, spread):
            dealt = sb_tile(name, [P, R], U8)
            nc.gpsimd.tensor_copy(
                dealt[:].rearrange("p (t m) -> p t m", t=PACK),
                spread[:].rearrange("p (m t) -> p t m", t=PACK),
            )
            return dealt

        warm = keep.tile([P, 2], F32, name="warm")
        nc.gpsimd.memset(warm[:, 0:1], 0.0)
        x_scales = sb_tile("x_scales", [P, T], U8)
        nc.vector.memset(x_scales[:].bitcast(I32), 0)
        w_spread = sb_tile("w_spread", [P, R], U8)
        nc.vector.memset(w_spread[:].bitcast(I32), 0)
        w2_spread = sb_tile("w2_spread", [P, R], U8)
        nc.gpsimd.memset(w2_spread[:].bitcast(I32), 0)

        x_staged = [sb_tile("x_staged%d" % h, [P, 2, T // 4], I32) for h in range(2)]
        x_rows = xt_scales[0].bitcast(I32).rearrange("(h q r) c -> h r q c", h=2, q=2)
        nc.sync.dma_start(x_staged[0][0:PACK, :, :], x_rows[0])
        nc.scalar.dma_start(x_staged[1][2 * QUAD : 2 * QUAD + PACK, :, :], x_rows[1])
        list1 = load_list("list1", offs)
        w_staged = stage_scales("w_staged", w_scales, nc.scalar)
        w_raw = sb_tile("w_raw", [P, 2 * R], U8)
        nc.scalar.dma_start(w_raw[:].bitcast(I32), w_words[0].bitcast(I32))
        x_words = sb_tile("x_words", [P, T], U32)
        nc.scalar.dma_start(x_words[:].bitcast(I32), xt_words[0].rearrange("p c t -> p (c t)").bitcast(I32))
        nc.scalar.activation(warm[:, 1:2], warm[:, 0:1], ACT.Sigmoid)
        list3 = load_list("list3", offs3)
        w2_raw = sb_tile("w2_raw", [P, R], U32)
        nc.scalar.dma_start(w2_raw[:].bitcast(I32), w2_words[0].rearrange("p c t -> p (c t)").bitcast(I32))
        list2 = load_list("list2", offs2)
        load_scale_rows(w2_spread, w2_scales)
        list6 = load_list("list6", offs6)
        list5 = load_list("list5", offs5)
        sg_col = load_rows("sg_col", sg)
        bg_col = load_rows("bg_col", bg)
        sa_col = load_rows("sa_col", sa)
        list4 = load_list("list4", offs4)
        list7 = load_list("list7", offs7)
        sb_col = load_rows("sb_col", sb)
        wb_codes = sb_tile("wb_codes", [P, 2 * N], U8)
        nc.sync.dma_start(wb_codes[:].bitcast(I32), wb_words[0].bitcast(I32))

        board_w = [keep.tile([P, C], F32, name="board_w%d" % t) for t in range(PACK)]
        for t in range(PACK):
            (nc.vector if t < 2 else nc.gpsimd).memset(board_w[t][:], 0.0)

        for q in range(PACK):
            nc.vector.tensor_copy(w_spread[QUAD * q : QUAD * q + PACK, :].bitcast(I32), w_staged[:, q, :])
        w_dealt_scales = deal_scales("w_dealt_scales", w_spread)
        for q in range(PACK):
            src = 2 * QUAD * (q // 2)
            nc.vector.tensor_copy(x_scales[QUAD * q : QUAD * q + PACK, :].bitcast(I32), x_staged[q // 2][src : src + PACK, q % 2, :])
        w_dealt = sb_tile("w_dealt", [P, 2 * R], U8)
        nc.scalar.copy(
            w_dealt[:].bitcast(U16).rearrange("p (t m) -> p t m", t=PACK),
            w_raw[:].bitcast(U16).rearrange("p (m t) -> p t m", t=PACK),
        )

        x1_scales = sb_tile("x1_scales", [P, J], U8)
        nc.vector.tensor_copy(x1_scales[:], x_scales[:].indirect(list1[:]))
        x1_words = sb_tile("x1_words", [P, J], U32)
        nc.vector.tensor_copy(x1_words[:], x_words[:].indirect(list1[:]))
        x2_scales = sb_tile("x2_scales", [P, J], U8)
        nc.vector.tensor_copy(x2_scales[:], x_scales[:].indirect(list2[:]))
        w2_dealt_scales = deal_scales("w2_dealt_scales", w2_spread)

        w2_dealt = sb_tile("w2_dealt", [P, R], U32)
        nc.gpsimd.tensor_copy(
            w2_dealt[:].rearrange("p (t m) -> p t m", t=PACK),
            w2_raw[:].rearrange("p (m t) -> p t m", t=PACK),
        )
        x2_words = sb_tile("x2_words", [P, J], U32)
        nc.vector.tensor_copy(x2_words[:], x_words[:].indirect(list2[:]))

        wb_plane = sb_tile("wb_plane", [P, N], U8)
        nc.gpsimd.memset(wb_plane[:].bitcast(I32), 0)
        load_scale_rows(wb_plane, wb_scales)

        a_sums = [psum.tile([P, J], F32, name="a_sums%d" % t, tag="bank%d" % t) for t in range(PACK)]
        b_pair = psum.tile([P, 2, J], F32, name="b_pair")
        b_sums = [b_pair[:, 0, :], b_pair[:, 1, :]] + [psum.tile([P, J], F32, name="b_sums%d" % t)[:] for t in (2, 3)]
        for t in (1, 0, 3, 2):
            nc.tensor.matmul_mx(
                out=a_sums[t][:],
                lhsT=w_dealt[:, 2 * P * t : 2 * P * (t + 1)].bitcast(E2M1),
                lhsT_scale=w_dealt_scales[:, P * t : P * (t + 1)],
                rhs=x1_words[:].bitcast(E5M2), rhs_scale=x1_scales[:], start=True, stop=True,
            )
        for t in range(PACK):
            nc.tensor.matmul_mx(
                out=b_sums[t],
                lhsT=w2_dealt[:, P * t : P * (t + 1)].bitcast(E4M3),
                lhsT_scale=w2_dealt_scales[:, P * t : P * (t + 1)],
                rhs=x2_words[:].bitcast(E5M2), rhs_scale=x2_scales[:], start=True, stop=True,
            )
        spent = ["w_dealt", "w_dealt_scales", "w2_dealt", "w2_dealt_scales"]
        board_v = [sb_tile("board_v%d" % t, [P, C], F32, tag=spent[t]) for t in range(PACK)]
        for t in range(PACK):
            nc.gpsimd.memset(board_v[t][:], 0.0)

        a_rows = [keep.tile([P, J], F32, name="a_rows%d" % t) for t in range(PACK)]
        b_pair_rows = keep.tile([P, 2, J], F32, name="b_pair_rows")
        b_rows = [b_pair_rows[:, 0, :], b_pair_rows[:, 1, :]] + [keep.tile([P, J], F32, name="b_rows%d" % t)[:] for t in (2, 3)]
        first = keep.tile([P, PACK, O], F32, name="first")
        gate = keep.tile([P, PACK, O], F32, name="gate")
        second = keep.tile([P, PACK, O], F32, name="second")

        def put(engine, board, lst, rows):
            if engine == "vector":
                nc.vector.tensor_copy(board[:].indirect(lst[:]), rows)
            else:
                nc.scalar.activation(board[:].indirect(lst[:]), rows, ACT.Copy)

        def look_w(t):
            nc.scalar.activation(gate[:, t, :], board_w[t][:].indirect(list6[:]), ACT.Sigmoid,
                                 bias=bg_col[:, t : t + 1], scale=sg_col[:, t : t + 1])
            nc.scalar.activation(first[:, t, :], board_w[t][:].indirect(list5[:]), ACT.Copy,
                                 scale=sa_col[:, t : t + 1])

        def look_v(t):
            nc.scalar.activation(second[:, t, :], board_v[t][:].indirect(list7[:]), ACT.Copy,
                                 scale=sb_col[:, t : t + 1])

        nc.scalar.copy(a_rows[1][:], a_sums[1][:])
        nc.scalar.copy(a_rows[0][:], a_sums[0][:])
        put("scalar", board_w[1], list3, a_rows[1][:])
        put("vector", board_w[0], list3, a_rows[0][:])
        nc.scalar.copy(a_rows[3][:], a_sums[3][:])
        nc.vector.tensor_copy(a_rows[2][:], a_sums[2][:])
        put("scalar", board_w[3], list3, a_rows[3][:])
        put("vector", board_w[2], list3, a_rows[2][:])
        nc.vector.tensor_copy(b_pair_rows[:], b_pair[:])
        nc.vector.tensor_copy(b_rows[3], b_sums[3])
        nc.scalar.copy(b_rows[2], b_sums[2])
        for t in range(PACK):
            look_w(t)
        put("vector", board_v[0], list4, b_rows[0])
        put("vector", board_v[1], list4, b_rows[1])
        put("scalar", board_v[2], list4, b_rows[2])
        put("vector", board_v[3], list4, b_rows[3])
        gated = keep.tile([P, PACK, O], F32, name="gated")
        nc.gpsimd.tensor_tensor(gated[:], first[:], gate[:], ALU.mult)
        for t in range(PACK):
            look_v(t)

        larger = keep.tile([P, PACK, O], F32, name="larger")
        nc.vector.tensor_tensor(larger[:, : PACK - 1, :], gated[:, : PACK - 1, :], second[:, : PACK - 1, :], ALU.max)
        nc.vector.tensor_tensor(larger[:, PACK - 1, :], gated[:, PACK - 1, :], second[:, PACK - 1, :], ALU.max)
        hid = sb_tile("hid", [P, O * PACK], BF16)
        nc.vector.tensor_copy(hid[:].rearrange("p (o t) -> p o t", t=PACK), larger[:].rearrange("p t o -> p o t"))
        hid_codes = sb_tile("hid_codes", [P, O], U32)
        hid_scales = sb_tile("hid_scales", [P, O], U8)
        nc.vector.quantize_mx(out=hid_codes[:].bitcast(E4M3), scales=hid_scales[:], in_=hid[:])

        for h in range(N // P):
            y_sums = psum.tile([P, O], F32, name="y_sums%d" % h, tag="bank%d" % h)
            nc.tensor.matmul_mx(
                out=y_sums[:],
                lhsT=wb_codes[:, 2 * P * h : 2 * P * (h + 1)].bitcast(E2M1),
                lhsT_scale=wb_plane[:, P * h : P * (h + 1)],
                rhs=hid_codes[:].bitcast(E4M3), rhs_scale=hid_scales[:], start=True, stop=True,
            )
            y_rows = keep.tile([P, O], F32, name="y_rows%d" % h)
            if h == 0:
                nc.scalar.copy(y_rows[:], y_sums[:])
                nc.scalar.dma_start(out[P * h : P * (h + 1), :], y_rows[:])
            else:
                nc.vector.tensor_copy(y_rows[:], y_sums[:])
                nc.sync.dma_start(out[P * h : P * (h + 1), :], y_rows[:])
